import numpy as np, ml_dtypes
CORES = [3,7,11,15,131,135,139,143]
N = 8
KB, QP, ROOT = 1, 64, 4
def setup_inputs(rng):
    return {"q": rng.standard_normal((N, 128, QP), dtype=np.float32).astype(ml_dtypes.bfloat16), "k": rng.standard_normal((N, 128, KB * 128), dtype=np.float32).astype(ml_dtypes.bfloat16), "v": rng.standard_normal((N, 128, KB * 128), dtype=np.float32).astype(ml_dtypes.bfloat16)}
def setup_inputs_big(rng):
    d = setup_inputs(rng)
    for k in ("q", "k", "v"): d[k] = (d[k].astype(np.float32) * 1024.0).astype(d[k].dtype)
    return d
def setup_inputs_small(rng):
    d = setup_inputs(rng)
    for k in ("q", "k", "v"): d[k] = (d[k].astype(np.float32) * (1 / 1024.0)).astype(d[k].dtype)
    return d
def setup_inputs_apart(rng):
    d = setup_inputs(rng)
    f = (10.0 ** rng.permutation(np.linspace(-1.5, 1.5, N))).astype(np.float32).reshape(N, 1, 1)
    for k in ("q", "k", "v"): d[k] = (d[k].astype(np.float32) * f).astype(d[k].dtype)
    return d
def reference(q, k, v):
    Q, K, V = q.astype(np.float64), k.astype(np.float64), v.astype(np.float64)
    o = np.zeros((128, QP))
    for j in range(N):
        for b in range(KB):
            o += V[j][:, 128 * b:128 * b + 128].T @ np.maximum(K[j][:, 128 * b:128 * b + 128].T @ Q[ROOT], 0.0)
    y = np.full((N, 128, QP), np.nan)
    y[ROOT] = o
    return {"y": y.astype(ml_dtypes.bfloat16 if q.dtype != np.float64 else np.float64)}

@@ -1,0 +1,103 @@
+from concourse.mybir import dt, AluOpType
+
+KV = 256
+QP = 64
+NBANK = 4
+
+SCRATCH = {
+    "land": ("sbuf", [128, 8 * KV], "bfloat16"),
+    "qs": ("sbuf", [128, QP], "bfloat16"),
+    "zero": ("sbuf", [128, QP], "float32"),
+    "ssb": ("sbuf", [128, 8 * QP], "bfloat16"),
+    "ysb": ("sbuf", [128, QP], "bfloat16"),
+    "ps0": ("psum", [128, 512], "float32"),
+    "ps1": ("psum", [128, 512], "float32"),
+    "ps2": ("psum", [128, 512], "float32"),
+    "ps3": ("psum", [128, 512], "float32"),
+    "po": ("psum", [128, 512], "float32"),
+}
+SEMAPHORES = (["ld", "ldq", "sent", "zs", "od", "yc", "st"]
+              + ["arr%d" % j for j in range(8)] + ["s%d" % j for j in range(8)] + ["r%d" % j for j in range(8)])
+
+
+def _bits(m):
+    return bin(m).count("1")
+
+
+def _distance(topo, a, b):
+    if a == b:
+        return 0
+    if topo.host(a) == topo.host(b) and topo.chip(a) == topo.chip(b):
+        return 1
+    if topo.mates(a, b):
+        return 2
+    if topo.same_plane(a, b):
+        return 3
+    return 4
+
+
+def rank_program(g, core, T, topo):
+    rank = T.rank_of(core)
+    if rank is None:
+        return
+    sem = T.sem
+    root = T.root
+    root_core = T.cores[root]
+    n = len(T.cores)
+
+    def kslot(j):
+        return T.land[:, j * KV:j * KV + 128]
+
+    def vslot(j):
+        return T.land[:, j * KV + 128:(j + 1) * KV]
+
+    def slot(j):
+        return T.land[:, j * KV:(j + 1) * KV]
+
+    if rank != root:
+        g.sync.dma_start(kslot(rank), T.k[:, :]).then_inc(sem.ld, 16)
+        g.scalar.dma_start(vslot(rank), T.v[:, :]).then_inc(sem.ld, 16)
+        m = topo.mask(core, root_core)
+        rid, pid = topo.addr(root_core, core)
+        g.wait_ge(sem.ld, 32)
+        g.remote_dma(out_ap=slot(rank), in_ap=slot(rank), remote_sem=sem["arr%d" % rank], local_sem=sem.sent,
+                     pid=pid, routing_id=rid, dma_engine_mask=m)
+        g.wait_ge(sem.sent, _bits(m))
+        return
+
+    order = sorted(range(n), key=lambda j: (_distance(topo, T.cores[j], root_core), j))
+    banks = [T.ps0, T.ps1, T.ps2, T.ps3]
+
+    g.sync.dma_start(T.qs[:, :], T.q[:, :]).then_inc(sem.ldq, 16)
+    g.scalar.dma_start(kslot(root), T.k[:, :]).then_inc(sem.ld, 16)
+    g.sync.dma_start(vslot(root), T.v[:, :]).then_inc(sem.ld, 16)
+
+    g.vector.memset(T.zero[:, :], 0.0).then_inc(sem.zs, 1)
+    g.vector.wait_ge(sem.zs, 1)
+
+    def emit_o(i):
+        j = order[i]
+        g.tensor.wait_ge(sem["r%d" % i], 1)
+        mm = g.tensor.matmul(T.po[:, 0:QP], vslot(j), T.ssb[:, i * QP:(i + 1) * QP], i == 0, i == n - 1)
+        if i == n - 1:
+            mm.then_inc(sem.od, 1)
+
+    g.tensor.wait_ge(sem.ldq, 16)
+    for i, j in enumerate(order):
+        if j == root:
+            g.tensor.wait_ge(sem.ld, 32)
+        else:
+            g.tensor.wait_ge(sem["arr%d" % j], _bits(topo.mask(T.cores[j], root_core)))
+        g.tensor.matmul(banks[i % NBANK][:, 0:QP], kslot(j), T.qs[:, :], True, True).then_inc(sem["s%d" % i], 1)
+        g.vector.wait_ge(sem["s%d" % i], 1)
+        g.vector.tensor_tensor(T.ssb[:, i * QP:(i + 1) * QP], banks[i % NBANK][:, 0:QP], T.zero[:, :],
+                               AluOpType.max).then_inc(sem["r%d" % i], 1)
+        if i >= 1:
+            emit_o(i - 1)
+    emit_o(n - 1)
+
+    g.vector.wait_ge(sem.od, 1)
+    g.vector.tensor_copy(T.ysb[:, :], T.po[:, 0:QP]).then_inc(sem.yc, 1)
+    g.sync.wait_ge(sem.yc, 1)
+    g.sync.dma_start(T.y[:, :], T.ysb[:, :]).then_inc(sem.st, 16)
+    g.sync.wait_ge(sem.st, 16)

@@ -16,8 +16,9 @@ SCRATCH = {
     "ps3": ("psum", [128, 512], "float32"),
     "po": ("psum", [128, 512], "float32"),
 }
-SEMAPHORES = (["ld", "ldq", "sent", "zs", "od", "yc", "st"]
-              + ["arr%d" % j for j in range(8)] + ["s%d" % j for j in range(8)] + ["r%d" % j for j in range(8)])
+SEMAPHORES = (["lk", "lv", "ldq", "sent", "zs", "od", "yc", "st"]
+              + ["ak%d" % j for j in range(8)] + ["av%d" % j for j in range(8)]
+              + ["s%d" % j for j in range(8)] + ["r%d" % j for j in range(8)])
 
 
 def _bits(m):
@@ -51,50 +52,51 @@ def rank_program(g, core, T, topo):
     def vslot(j):
         return T.land[:, j * KV + 128:(j + 1) * KV]
 
-    def slot(j):
-        return T.land[:, j * KV:(j + 1) * KV]
+    g.sync.dma_start(kslot(rank), T.k[:, :]).then_inc(sem.lk, 16)
+    g.scalar.dma_start(vslot(rank), T.v[:, :]).then_inc(sem.lv, 16)
 
     if rank != root:
-        g.sync.dma_start(kslot(rank), T.k[:, :]).then_inc(sem.ld, 16)
-        g.scalar.dma_start(vslot(rank), T.v[:, :]).then_inc(sem.ld, 16)
         m = topo.mask(core, root_core)
         rid, pid = topo.addr(root_core, core)
-        g.wait_ge(sem.ld, 32)
-        g.remote_dma(out_ap=slot(rank), in_ap=slot(rank), remote_sem=sem["arr%d" % rank], local_sem=sem.sent,
+        g.wait_ge(sem.lk, 16)
+        g.remote_dma(out_ap=kslot(rank), in_ap=kslot(rank), remote_sem=sem["ak%d" % rank], local_sem=sem.sent,
                      pid=pid, routing_id=rid, dma_engine_mask=m)
-        g.wait_ge(sem.sent, _bits(m))
+        g.wait_ge(sem.lv, 16)
+        g.remote_dma(out_ap=vslot(rank), in_ap=vslot(rank), remote_sem=sem["av%d" % rank], local_sem=sem.sent,
+                     pid=pid, routing_id=rid, dma_engine_mask=m)
+        g.wait_ge(sem.sent, 2 * _bits(m))
         return
 
     order = sorted(range(n), key=lambda j: (_distance(topo, T.cores[j], root_core), j))
     banks = [T.ps0, T.ps1, T.ps2, T.ps3]
 
     g.sync.dma_start(T.qs[:, :], T.q[:, :]).then_inc(sem.ldq, 16)
-    g.scalar.dma_start(kslot(root), T.k[:, :]).then_inc(sem.ld, 16)
-    g.sync.dma_start(vslot(root), T.v[:, :]).then_inc(sem.ld, 16)
-
     g.vector.memset(T.zero[:, :], 0.0).then_inc(sem.zs, 1)
     g.vector.wait_ge(sem.zs, 1)
 
-    def emit_o(i):
-        j = order[i]
-        g.tensor.wait_ge(sem["r%d" % i], 1)
-        mm = g.tensor.matmul(T.po[:, 0:QP], vslot(j), T.ssb[:, i * QP:(i + 1) * QP], i == 0, i == n - 1)
-        if i == n - 1:
-            mm.then_inc(sem.od, 1)
+    def wait_for(j, own, far):
+        if j == root:
+            g.tensor.wait_ge(sem[own], 16)
+        else:
+            g.tensor.wait_ge(sem["%s%d" % (far, j)], _bits(topo.mask(T.cores[j], root_core)))
 
     g.tensor.wait_ge(sem.ldq, 16)
-    for i, j in enumerate(order):
-        if j == root:
-            g.tensor.wait_ge(sem.ld, 32)
-        else:
-            g.tensor.wait_ge(sem["arr%d" % j], _bits(topo.mask(T.cores[j], root_core)))
-        g.tensor.matmul(banks[i % NBANK][:, 0:QP], kslot(j), T.qs[:, :], True, True).then_inc(sem["s%d" % i], 1)
-        g.vector.wait_ge(sem["s%d" % i], 1)
-        g.vector.tensor_tensor(T.ssb[:, i * QP:(i + 1) * QP], banks[i % NBANK][:, 0:QP], T.zero[:, :],
-                               AluOpType.max).then_inc(sem["r%d" % i], 1)
-        if i >= 1:
-            emit_o(i - 1)
-    emit_o(n - 1)
+    for lo in range(0, n, NBANK):
+        group = range(lo, min(lo + NBANK, n))
+        for i in group:
+            j = order[i]
+            wait_for(j, "lk", "ak")
+            g.tensor.matmul(banks[i % NBANK][:, 0:QP], kslot(j), T.qs[:, :], True, True).then_inc(sem["s%d" % i], 1)
+            g.vector.wait_ge(sem["s%d" % i], 1)
+            g.vector.tensor_tensor(T.ssb[:, i * QP:(i + 1) * QP], banks[i % NBANK][:, 0:QP], T.zero[:, :],
+                                   AluOpType.max).then_inc(sem["r%d" % i], 1)
+        for i in group:
+            j = order[i]
+            wait_for(j, "lv", "av")
+            g.tensor.wait_ge(sem["r%d" % i], 1)
+            mm = g.tensor.matmul(T.po[:, 0:QP], vslot(j), T.ssb[:, i * QP:(i + 1) * QP], i == 0, i == n - 1)
+            if i == n - 1:
+                mm.then_inc(sem.od, 1)
 
     g.vector.wait_ge(sem.od, 1)
     g.vector.tensor_copy(T.ysb[:, :], T.po[:, 0:QP]).then_inc(sem.yc, 1)

from concourse.mybir import dt, AluOpType

KV = 256
QP = 64
NBANK = 4

SCRATCH = {
    "land": ("sbuf", [128, 8 * KV], "bfloat16"),
    "qs": ("sbuf", [128, QP], "bfloat16"),
    "zero": ("sbuf", [128, QP], "float32"),
    "ssb": ("sbuf", [128, 8 * QP], "bfloat16"),
    "ysb": ("sbuf", [128, QP], "bfloat16"),
    "ps0": ("psum", [128, 512], "float32"),
    "ps1": ("psum", [128, 512], "float32"),
    "ps2": ("psum", [128, 512], "float32"),
    "ps3": ("psum", [128, 512], "float32"),
    "po": ("psum", [128, 512], "float32"),
}
SEMAPHORES = (["lk", "lv", "ldq", "sent", "zs", "od", "yc", "st"]
              + ["ak%d" % j for j in range(8)] + ["av%d" % j for j in range(8)]
              + ["s%d" % j for j in range(8)] + ["r%d" % j for j in range(8)])


def _bits(m):
    return bin(m).count("1")


def _distance(topo, a, b):
    if a == b:
        return 0
    if topo.host(a) == topo.host(b) and topo.chip(a) == topo.chip(b):
        return 1
    if topo.mates(a, b):
        return 2
    if topo.same_plane(a, b):
        return 3
    return 4


def rank_program(g, core, T, topo):
    rank = T.rank_of(core)
    if rank is None:
        return
    sem = T.sem
    root = T.root
    root_core = T.cores[root]
    n = len(T.cores)

    def kslot(j):
        return T.land[:, j * KV:j * KV + 128]

    def vslot(j):
        return T.land[:, j * KV + 128:(j + 1) * KV]

    g.sync.dma_start(kslot(rank), T.k[:, :]).then_inc(sem.lk, 16)
    g.scalar.dma_start(vslot(rank), T.v[:, :]).then_inc(sem.lv, 16)

    if rank != root:
        m = topo.mask(core, root_core)
        rid, pid = topo.addr(root_core, core)
        g.wait_ge(sem.lk, 16)
        g.remote_dma(out_ap=kslot(rank), in_ap=kslot(rank), remote_sem=sem["ak%d" % rank], local_sem=sem.sent,
                     pid=pid, routing_id=rid, dma_engine_mask=m)
        g.wait_ge(sem.lv, 16)
        g.remote_dma(out_ap=vslot(rank), in_ap=vslot(rank), remote_sem=sem["av%d" % rank], local_sem=sem.sent,
                     pid=pid, routing_id=rid, dma_engine_mask=m)
        g.wait_ge(sem.sent, 2 * _bits(m))
        return

    order = sorted(range(n), key=lambda j: (_distance(topo, T.cores[j], root_core), j))
    banks = [T.ps0, T.ps1, T.ps2, T.ps3]

    g.sync.dma_start(T.qs[:, :], T.q[:, :]).then_inc(sem.ldq, 16)
    g.vector.memset(T.zero[:, :], 0.0).then_inc(sem.zs, 1)
    g.vector.wait_ge(sem.zs, 1)

    def wait_for(j, own, far):
        if j == root:
            g.tensor.wait_ge(sem[own], 16)
        else:
            g.tensor.wait_ge(sem["%s%d" % (far, j)], _bits(topo.mask(T.cores[j], root_core)))

    g.tensor.wait_ge(sem.ldq, 16)
    for lo in range(0, n, NBANK):
        group = range(lo, min(lo + NBANK, n))
        for i in group:
            j = order[i]
            wait_for(j, "lk", "ak")
            g.tensor.matmul(banks[i % NBANK][:, 0:QP], kslot(j), T.qs[:, :], True, True).then_inc(sem["s%d" % i], 1)
            g.vector.wait_ge(sem["s%d" % i], 1)
            g.vector.tensor_tensor(T.ssb[:, i * QP:(i + 1) * QP], banks[i % NBANK][:, 0:QP], T.zero[:, :],
                                   AluOpType.max).then_inc(sem["r%d" % i], 1)
        for i in group:
            j = order[i]
            wait_for(j, "lv", "av")
            g.tensor.wait_ge(sem["r%d" % i], 1)
            mm = g.tensor.matmul(T.po[:, 0:QP], vslot(j), T.ssb[:, i * QP:(i + 1) * QP], i == 0, i == n - 1)
            if i == n - 1:
                mm.then_inc(sem.od, 1)

    g.vector.wait_ge(sem.od, 1)
    g.vector.tensor_copy(T.ysb[:, :], T.po[:, 0:QP]).then_inc(sem.yc, 1)
    g.sync.wait_ge(sem.yc, 1)
    g.sync.dma_start(T.y[:, :], T.ysb[:, :]).then_inc(sem.st, 16)
    g.sync.wait_ge(sem.st, 16)
